import numpy as np
import ml_dtypes


def mxq(x, axis, fmt="e4m3"):
    dtype, down = {"e4m3": (ml_dtypes.float8_e4m3fn, 7), "e5m2": (ml_dtypes.float8_e5m2, 14)}[fmt]
    v = np.moveaxis(np.asarray(x, np.float32).astype(ml_dtypes.bfloat16).astype(np.float64), axis, -1)
    blocks = v.reshape(v.shape[:-1] + (-1, 32))
    amax = np.abs(blocks).max(-1, keepdims=True)
    byte = np.maximum(np.where(amax > 0, np.frexp(amax)[1] - 1 + 127, 0) - down, 1)
    scale = np.exp2(byte - 127.0)
    codes = (blocks / scale).astype(np.float32).astype(dtype).astype(np.float64)
    return np.moveaxis((codes * scale).reshape(v.shape), -1, axis)


WIDE = False


def mx_kscale(k):
    if not WIDE:
        return np.ones(k)
    levels = np.array([10, -10, 5, -5, 0])
    if k % 512:
        return np.exp2(np.random.permutation(np.resize(levels, k // 32))).repeat(32)
    a = np.empty((k // 512, 16))
    for p in range(k // 512):
        a[p, :8] = np.random.permutation(np.resize(levels, 8))
        for g in range(8):
            far = levels[np.abs(levels - a[p, g]) >= 10]
            a[p, g + 8] = far[np.random.randint(len(far))]
    return np.exp2(a.ravel()).repeat(32)


BF16 = ml_dtypes.bfloat16


def bf(x):
    return np.asarray(x, np.float32).astype(BF16)


def f64(x):
    return np.asarray(x).astype(np.float64)


E2M1 = np.array([0.0, 0.5, 1.0, 1.5, 2.0, 3.0, 4.0, 6.0, -0.0, -0.5, -1.0, -1.5, -2.0, -3.0, -4.0, -6.0])


def pack_weight(w, fmt):
    k, n = w.shape
    w = f64(bf(w)).reshape(k // 32, 32, n)
    amax = np.abs(w).max(1)
    if fmt == "e4m3":
        byte = np.frexp(amax)[1] - 1 + 127 - 7
    else:
        mant, ex = np.frexp(amax / 6.0)
        byte = np.where(mant > 0.5, ex, ex - 1) + 127
    byte = np.clip(np.where(amax > 0, byte, 1), 1, 254)
    scaled = (w * np.exp2(127.0 - byte)[:, None, :]).reshape(k, n).astype(np.float32)
    by_word = np.ascontiguousarray(scaled.reshape(k // 512, 128, 4, n).transpose(0, 1, 3, 2))
    if fmt == "e4m3":
        words = by_word.astype(ml_dtypes.float8_e4m3fn).view(np.uint8)
    else:
        c = by_word.astype(ml_dtypes.float4_e2m1fn).view(np.uint8) & 0xF
        words = c[..., 0::2] | (c[..., 1::2] << 4)
    return np.ascontiguousarray(words), np.ascontiguousarray(byte.astype(np.uint8).reshape(k // 512, 16, n))


def unpack_weight(words, scales, fmt):
    g, p, n, _ = words.shape
    if fmt == "e4m3":
        vals = np.ascontiguousarray(words).view(ml_dtypes.float8_e4m3fn).astype(np.float64)
    else:
        nib = np.empty((g, p, n, 4), np.uint8)
        nib[..., 0::2] = words & 0xF
        nib[..., 1::2] = words >> 4
        vals = E2M1[nib]
    vals = vals * np.repeat(np.exp2(scales.astype(np.float64) - 127.0), 8, axis=1)[..., None]
    return vals.transpose(0, 1, 3, 2).reshape(g * 512, n)
def pack4(w):
    words, scales = pack_weight(w, "e2m1")
    return words.reshape(words.shape[0], 128, -1), scales


def unpack4(words, scales):
    return unpack_weight(words.reshape(words.shape[0], 128, -1, 2), scales, "e2m1")


B, S, D, M, N, C = 2, 1024, 512, 512, 512, 2


def cauchy_parts(om, nu, b):
    de = om[:, None] - nu[None, :]
    w = b[None, :] / (0.25 + de * de)
    gr = 0.5 * w
    gi = -de * w
    return gr, gi


def draw0():
    s, t, r = mx_kscale(S), mx_kscale(M), mx_kscale(N)
    x = bf(np.random.standard_normal((B, S, D)) / s[None, :, None])
    p = np.random.standard_normal((M, S)) / np.sqrt(S) * s[None, :] * t[:, None]
    p_words, p_scales = pack4(p.T)
    om = bf(np.random.uniform(-4.0, 4.0, M))
    nu = bf(np.random.uniform(-4.0, 4.0, N))
    b = bf(np.random.standard_normal(N) * r)
    c = np.random.standard_normal((N, D)) * 1.5 / np.sqrt(N) / r[:, None]
    c_words, c_scales = pack4(c)
    q = bf(np.random.standard_normal((C, S, M)) / np.sqrt(M) / t[None, None, :])
    return {"x": x,
            "p_words": p_words,
            "p_scales": p_scales,
            "om": om,
            "nu": nu,
            "b": b,
            "c_words": c_words,
            "c_scales": c_scales,
            "q": q}


def core(x, p_words, p_scales, om, nu, b, c_words, c_scales, q):
    gr, gi = cauchy_parts(f64(om), f64(nu), f64(b))
    gr, gi = gr, gi
    cq = unpack4(c_words, c_scales)
    kr = mxq(gr, 1, "e4m3") @ cq
    ki = mxq(gi, 1, "e4m3") @ cq
    u = unpack4(p_words, p_scales).T @ mxq(f64(x), 1, "e4m3")
    fr = kr[None, :, :] * u
    fi = ki[None, :, :] * u
    qq = mxq(f64(q), 2, "e4m3")
    return (qq[0] @ mxq(fr, 1, "e4m3")) - (qq[1] @ mxq(fi, 1, "e4m3"))


def e4m3fn_bytes(y):
    return np.clip(np.asarray(y, np.float64), -448.0, 448.0).astype(np.float32).astype(ml_dtypes.float8_e4m3fn).view(np.uint8)


def e4m3fn_values(b):
    return np.asarray(b, np.uint8).view(ml_dtypes.float8_e4m3fn).astype(np.float64)


def setup_inputs():
    d = draw0()
    x0 = np.asarray(d['x']).astype(np.float64)
    s = (np.max(np.abs(x0), axis=(0, 2), keepdims=True) / 448.0).astype(np.float32)
    out = {}
    for k, v in d.items():
        if k == 'x':
            out['x_bytes'] = e4m3fn_bytes(x0 / s.astype(np.float64))
            out['x_scale'] = s
        else:
            out[k] = v
    return out


def reference(x_bytes, x_scale, p_words, p_scales, om, nu, b, c_words, c_scales, q):
    return core(e4m3fn_values(x_bytes) * x_scale.astype(np.float64), p_words, p_scales, om, nu, b, c_words, c_scales, q)

@@ -1,0 +1,502 @@
+from contextlib import ExitStack
+
+import concourse.mybir as mybir
+from concourse.masks import make_identity
+
+B, S, D, M, N, C = 2, 1024, 512, 512, 512, 2
+FLOPS = 2 * (2 * M * N * D + B * M * S * D + 2 * B * S * M * D)
+
+F32 = mybir.dt.float32
+BF16 = mybir.dt.bfloat16
+U32 = mybir.dt.uint32
+I32 = mybir.dt.int32
+U8 = mybir.dt.uint8
+F8 = mybir.dt.float8_e4m3fn
+E4M3 = mybir.dt.float8_e4m3fn_x4
+E2M1 = mybir.dt.float4_e2m1fn_x4
+ALU = mybir.AluOpType
+ACT = mybir.ActivationFunctionType
+
+P = 128
+T = 4
+G = S // 512
+CH = D // P
+J = S // P
+UNITS = [[(0, 256), (256, 512)], [(0, 256), (256, 384), (384, 512)]]
+
+
+def tile_cauchytransferfunctionfilter_w4_kernel(
+    tc, x_bytes, x_scale, p_words, p_scales, om, nu, b, c_words, c_scales, q, out
+):
+    nc = tc.nc
+    with ExitStack() as ctx:
+        keep = ctx.enter_context(tc.tile_pool(name="keep", bufs=1))
+        outp = ctx.enter_context(tc.tile_pool(name="outp", bufs=6))
+        psum = ctx.enter_context(tc.psum_pool(name="psum", bufs=4))
+
+        lhs_rows = keep.tile([P, N], BF16)
+        rhs_rows = keep.tile([P, M], BF16)
+        quarter = keep.tile([P, 1], F32)
+        warm = keep.tile([P, 1], F32)
+        p_scale_raw = keep.tile([P, G, M], U8, align_bytes=64)
+        c_scale = keep.tile([P, D], U8, align_bytes=64)
+        nc.vector.memset(rhs_rows[:].bitcast(F32), 0.0)
+        nc.gpsimd.memset(lhs_rows[:].bitcast(F32), 0.0)
+        nc.vector.memset(quarter[:], 0.25)
+        nc.vector.memset(rhs_rows[32:33, :], -1.0)
+        nc.vector.memset(lhs_rows[0:1, :], 1.0)
+        nc.scalar.activation(out=warm[:], in_=quarter[:], func=ACT.Abs_reciprocal_sqrt, bias=quarter[:], scale=1.0)
+        nc.vector.memset(p_scale_raw[:].rearrange("p g m -> p (g m)").bitcast(I32), 0)
+        nc.vector.memset(c_scale[:].bitcast(I32), 0)
+        b_col = keep.tile([P, T], BF16)
+        xs = keep.tile([P, G, T], F32)
+        p_raw = keep.tile([P, G, 2 * M], U8, align_bytes=64)
+        c_raw = keep.tile([P, 2 * D], U8, align_bytes=64)
+        q_raw = keep.tile([P, C, J, M], BF16, align_bytes=64)
+        x_raw = {}
+
+        def load_vectors():
+            nc.sync.dma_start(out=rhs_rows[0:1, :], in_=om.rearrange("(o m) -> o m", o=1))
+            nc.sync.dma_start(out=lhs_rows[32:33, :], in_=nu.rearrange("(o n) -> o n", o=1))
+            nc.sync.dma_start(out=xs[:], in_=x_scale.rearrange("o (g p t) w -> p (o g) (t w)", p=P, t=T))
+            nc.sync.dma_start(out=b_col[:], in_=b.rearrange("(p t) -> p t", t=T))
+
+        def load_x(i, g):
+            x_raw_t = keep.tile([P, T * D], U8, name="x_raw_%d_%d" % (i, g))
+            nc.sync.dma_start(
+                out=x_raw_t[:],
+                in_=x_bytes[i, g * 512 : (g + 1) * 512, :].rearrange("(p t) d -> p (t d)", t=T),
+            )
+            x_raw[i, g] = x_raw_t
+
+        def load_p():
+            nc.sync.dma_start(out=p_raw[:], in_=p_words.rearrange("g p w -> p g w"))
+
+        def load_p_scale():
+            for r4 in range(4):
+                nc.sync.dma_start(
+                    out=p_scale_raw[32 * r4 : 32 * r4 + 4, :, :].bitcast(I32),
+                    in_=p_scales[:, 4 * r4 : 4 * r4 + 4, :].rearrange("g q m -> q g m").bitcast(I32),
+                )
+
+        def load_c():
+            nc.sync.dma_start(out=c_raw[:], in_=c_words[0])
+
+        def load_c_scale():
+            for r4 in range(4):
+                nc.sync.dma_start(
+                    out=c_scale[32 * r4 : 32 * r4 + 4, :].bitcast(I32),
+                    in_=c_scales[0, 4 * r4 : 4 * r4 + 4, :].bitcast(I32),
+                )
+
+        def load_q(c, h):
+            nc.sync.dma_start(
+                out=q_raw[:, c, 4 * h : 4 * h + 4, :],
+                in_=q[c].rearrange("(p j) m -> p j m", j=J)[:, 4 * h : 4 * h + 4, :],
+            )
+
+        ident = keep.tile([P, P], F32)
+        make_identity(nc, ident[:])
+
+        ctx.enter_context(tc.manual_schedule())
+        r = keep.tile([P, T, M], F32)
+        w = keep.tile([P, T, M], F32)
+        de = {}
+
+        def make_de(tm):
+            de_ps = psum.tile([P, T, P], F32, tag="u")
+            de[tm] = de_ps
+            for t in range(T):
+                nc.tensor.matmul(
+                    out=de_ps[:, t, :], lhsT=lhs_rows[:, t::T], rhs=rhs_rows[:, tm::T], start=True, stop=True
+                )
+
+        def square(tm):
+            nc.scalar.activation(out=r[:, :, P * tm : P * (tm + 1)], in_=de[tm][:], func=ACT.Square)
+
+        def make_r(h):
+            cols = slice(256 * h, 256 * (h + 1))
+            nc.scalar.activation(
+                out=r[:, :, cols], in_=r[:, :, cols], func=ACT.Abs_reciprocal_sqrt, bias=quarter[:], scale=1.0
+            )
+
+        def make_w(h):
+            cols = slice(256 * h, 256 * (h + 1))
+            for t in range(T):
+                nc.vector.scalar_tensor_tensor(
+                    out=w[:, t, cols],
+                    in0=r[:, t, cols],
+                    scalar=b_col[:, t : t + 1],
+                    in1=r[:, t, cols],
+                    op0=ALU.mult,
+                    op1=ALU.mult,
+                )
+
+        g_bf, g_codes, g_scale = {}, {}, {}
+        for k in ("r", "i"):
+            g_bf_t = keep.tile([P, M, T], BF16, name="g_bf_" + k, align_bytes=64)
+            g_codes_t = keep.tile([P, M], U32, name="g_codes_" + k, align_bytes=64)
+            g_scale_t = keep.tile([P, M], U8, name="g_scale_" + k, align_bytes=64)
+            g_bf[k], g_codes[k], g_scale[k] = g_bf_t, g_codes_t, g_scale_t
+
+        w_mt = w[:].rearrange("p t m -> p m t")
+
+        def make_gr(h):
+            cols = slice(256 * h, 256 * (h + 1))
+            nc.vector.tensor_scalar(
+                out=g_bf["r"][:, cols, :], in0=w_mt[:, cols, :], scalar1=0.5, scalar2=None, op0=ALU.mult
+            )
+
+        def make_gi(tm):
+            sub = slice(P * tm, P * (tm + 1))
+            nc.vector.tensor_tensor(
+                out=g_bf["i"][:, sub, :],
+                in0=de[tm][:].rearrange("p t m -> p m t"),
+                in1=w_mt[:, sub, :],
+                op=ALU.mult,
+            )
+
+        def quant_g(k, h):
+            cols = slice(256 * h, 256 * (h + 1))
+            nc.vector.quantize_mx(
+                out=g_codes[k][:, cols].bitcast(E4M3),
+                scales=g_scale[k][:, cols],
+                in_=g_bf[k][:, cols, :].rearrange("p m t -> p (m t)"),
+            )
+
+        p_perm = keep.tile([P, G, 2 * M], U8, align_bytes=64)
+        p_scale = keep.tile([P, G, M], U8, align_bytes=64)
+
+        def make_p(g):
+            nc.vector.tensor_copy(
+                out=p_perm[:, g, :].rearrange("p (t m e) -> p t m e", t=T, e=2),
+                in_=p_raw[:, g, :].rearrange("p (m t e) -> p t m e", t=T, e=2),
+            )
+
+        def make_p_scale(g):
+            nc.vector.tensor_copy(
+                out=p_scale[:, g, :].rearrange("p (t m) -> p t m", t=T),
+                in_=p_scale_raw[:, g, :].rearrange("p (m t) -> p t m", t=T),
+            )
+
+        x_codes, x_sc = {}, {}
+
+        wide, inter = {}, {}
+
+        for i in range(B):
+            for g in range(G):
+                wide_t = keep.tile([P, T, D], BF16, name="wide_%d_%d" % (i, g), align_bytes=64)
+                wide[i, g] = wide_t
+
+        def widen_x(i, g, t, engine):
+            src = x_raw[i, g][:, t * D : (t + 1) * D].bitcast(F8)
+            scale = xs[:, g, t : t + 1]
+            dst = wide[i, g][:, t, :]
+            if engine == "v":
+                nc.vector.tensor_scalar(out=dst, in0=src, scalar1=scale, scalar2=None, op0=ALU.mult)
+            else:
+                nc.scalar.activation(out=dst, in_=src, func=ACT.Copy, scale=scale)
+
+        def drain(out_view, in_view, engine):
+            if engine == "v":
+                nc.vector.tensor_copy(out=out_view, in_=in_view)
+            else:
+                nc.scalar.copy(out=out_view, in_=in_view)
+
+        for i in range(B):
+            for g in range(G):
+                inter_t = keep.tile([P, D, T], BF16, name="inter_%d_%d" % (i, g), align_bytes=64)
+                inter[i, g] = inter_t
+
+        def inter_x(i, g, h):
+            cols = slice(256 * h, 256 * (h + 1))
+            nc.vector.tensor_copy(out=inter[i, g][:, cols, :], in_=wide[i, g][:, :, cols].rearrange("p t d -> p d t"))
+
+        def quant_x(i, g):
+            x_codes_t = keep.tile([P, D], U32, name="x_codes_%d_%d" % (i, g), align_bytes=64)
+            x_sc_t = keep.tile([P, D], U8, name="x_sc_%d_%d" % (i, g), align_bytes=64)
+            nc.vector.quantize_mx(
+                out=x_codes_t[:].bitcast(E4M3), scales=x_sc_t[:], in_=inter[i, g][:].rearrange("p d t -> p (d t)")
+            )
+            x_codes[i, g], x_sc[i, g] = x_codes_t, x_sc_t
+
+        q_codes = keep.tile([P, C, S], U32, align_bytes=64)
+        q_sc = keep.tile([P, C, S], U8, align_bytes=64)
+        q_bf = keep.tile([P, C, S, T], BF16, align_bytes=64)
+
+        q_ps = {}
+
+        def turn_q(c, jj):
+            bank = psum.tile([P, 2, 2, P], F32, tag="a", name="q_ps")
+            q_ps[c, jj] = bank
+            words = q_raw[:, c, :, :].rearrange("p j m -> p (j m)").bitcast(F32)
+            for k in range(2):
+                for u in range(2):
+                    base = (2 * jj + k) * (M // 2)
+                    nc.tensor.transpose(bank[:, k, u, :], words[:, base + u : base + M // 2 : 2], ident[:])
+
+        def drain_q(c, jj, engine):
+            drain(
+                q_bf[:, c, 2 * jj * P : (2 * jj + 2) * P, :]
+                .rearrange("p s t -> p (s t)")
+                .bitcast(F32)
+                .rearrange("p (k s u) -> p k s u", k=2, u=2),
+                q_ps[c, jj][:].rearrange("p k u s -> p k s u"),
+                engine,
+            )
+
+        def quant_q(c, h):
+            rows = slice(h * 512, (h + 1) * 512)
+            nc.vector.quantize_mx(
+                out=q_codes[:, c, rows].bitcast(E4M3),
+                scales=q_sc[:, c, rows],
+                in_=q_bf[:, c, rows, :].rearrange("p s t -> p (s t)"),
+            )
+
+        k_sb = keep.tile([P, 2, CH, P, T], F32)
+        k_ps = {}
+
+        def make_k(k, ch):
+            bank = psum.tile([P, T, P], F32, tag="a", name="k_ps")
+            k_ps[k, ch] = bank
+            for t in range(T):
+                cols = slice(t * P, (t + 1) * P)
+                nc.tensor.matmul_mx(
+                    out=bank[:, t, :],
+                    lhsT=g_codes[k][:, cols].bitcast(E4M3),
+                    lhsT_scale=g_scale[k][:, cols],
+                    rhs=c_raw[:, 2 * P * ch : 2 * P * (ch + 1)].bitcast(E2M1),
+                    rhs_scale=c_scale[:, P * ch : P * (ch + 1)],
+                    start=True,
+                    stop=True,
+                )
+
+        def drain_k(k, ch, engine):
+            drain(k_sb[:, 0 if k == "r" else 1, ch, :, :], k_ps[k, ch][:].rearrange("p t d -> p d t"), engine)
+
+        f_bf, f_codes, f_sc = {}, {}, {}
+        for i in range(B):
+            for d0, d1 in UNITS[i]:
+                f_bf_t = keep.tile([P, 2, d1 - d0, T], BF16, name="f_bf_%d_%d" % (i, d0), align_bytes=64)
+                f_codes_t = keep.tile([P, 2, d1 - d0], U32, name="f_codes_%d_%d" % (i, d0), align_bytes=64)
+                f_sc_t = keep.tile([P, 2, d1 - d0], U8, name="f_sc_%d_%d" % (i, d0), align_bytes=64)
+                f_bf[i, d0], f_codes[i, d0], f_sc[i, d0] = f_bf_t, f_codes_t, f_sc_t
+        u_ps = {}
+
+        def make_u(i, ch):
+            bank = psum.tile([P, T, P], F32, tag="u", name="u_ps")
+            u_ps[i, ch] = bank
+            for t in range(T):
+                for g in range(G):
+                    nc.tensor.matmul_mx(
+                        out=bank[:, t, :],
+                        lhsT=p_perm[:, g, 2 * P * t : 2 * P * (t + 1)].bitcast(E2M1),
+                        lhsT_scale=p_scale[:, g, P * t : P * (t + 1)],
+                        rhs=x_codes[i, g][:, P * ch : P * (ch + 1)].bitcast(E4M3),
+                        rhs_scale=x_sc[i, g][:, P * ch : P * (ch + 1)],
+                        start=(g == 0),
+                        stop=(g == G - 1),
+                    )
+
+        def make_f(i, d0, ch):
+            nc.vector.tensor_tensor(
+                out=f_bf[i, d0][:, :, P * ch - d0 : P * (ch + 1) - d0, :],
+                in0=u_ps[i, ch][:].rearrange("p (o t) d -> p o d t", o=1).to_broadcast([P, 2, P, T]),
+                in1=k_sb[:, :, ch, :, :],
+                op=ALU.mult,
+            )
+
+        def quant_f(i, d0):
+            nc.vector.quantize_mx(
+                out=f_codes[i, d0][:].rearrange("p k d -> p (k d)").bitcast(E4M3),
+                scales=f_sc[i, d0][:].rearrange("p k d -> p (k d)"),
+                in_=f_bf[i, d0][:].rearrange("p k d t -> p (k d t)"),
+            )
+
+        o_ps = {}
+
+        def synth(i, d0, d1, jj):
+            width = d1 - d0
+            tiles = 512 // width
+            bank = psum.tile([P, tiles, width], F32, tag="a", name="o_ps")
+            for kk in range(tiles):
+                j = tiles * jj + kk
+                for c in range(C):
+                    cols = slice(j * P, (j + 1) * P)
+                    nc.tensor.matmul_mx(
+                        out=bank[:, kk, :],
+                        lhsT=q_codes[:, c, cols].bitcast(E4M3),
+                        lhsT_scale=q_sc[:, c, cols],
+                        rhs=f_codes[i, d0][:, c, :].bitcast(E4M3),
+                        rhs_scale=f_sc[i, d0][:, c, :],
+                        start=(c == 0),
+                        stop=(c == C - 1),
+                    )
+            o_ps[i, d0, jj] = bank
+
+        def store(i, d0, d1, jj, engine):
+            tiles = 512 // (d1 - d0)
+            bank = o_ps[i, d0, jj]
+            o_sb = outp.tile([P, 512], F32)
+            o_view = o_sb[:].rearrange("p (k d) -> p k d", k=tiles)
+            drain(o_view, bank[:], engine)
+            nc.sync.dma_start(
+                out=out[i].rearrange("(p j) d -> p j d", j=J)[:, tiles * jj : tiles * (jj + 1), d0:d1], in_=o_view
+            )
+
+        load_x(0, 1)
+        load_vectors()
+        widen_x(0, 1, 3, "v")
+        make_de(0)
+        load_p()
+        widen_x(0, 1, 1, "s")
+        widen_x(0, 1, 2, "v")
+        widen_x(0, 1, 0, "s")
+        load_q(1, 0)
+        make_p(1)
+        make_de(1)
+        square(1)
+        load_q(0, 0)
+        load_p_scale()
+        make_p(0)
+        inter_x(0, 1, 0)
+        make_de(3)
+        inter_x(0, 1, 1)
+        turn_q(1, 1)
+        make_de(2)
+        square(0)
+        load_x(0, 0)
+        make_p_scale(1)
+        make_r(0)
+        square(3)
+        make_p_scale(0)
+        load_q(0, 1)
+        make_w(0)
+        square(2)
+        load_c_scale()
+        quant_x(0, 1)
+        turn_q(0, 0)
+        make_r(1)
+        load_x(1, 0)
+        drain_q(1, 1, "s")
+        widen_x(0, 0, 2, "s")
+        widen_x(0, 0, 1, "s")
+        make_gr(0)
+        widen_x(1, 0, 1, "s")
+        make_w(1)
+        load_c()
+        make_gi(0)
+        widen_x(0, 0, 0, "s")
+        quant_g("r", 0)
+        turn_q(1, 0)
+        widen_x(0, 0, 3, "s")
+        make_gi(1)
+        turn_q(0, 3)
+        make_gr(1)
+        turn_q(0, 1)
+        drain_q(0, 0, "s")
+        widen_x(1, 0, 2, "s")
+        make_gi(3)
+        drain_q(0, 3, "s")
+        inter_x(0, 0, 0)
+        drain_q(1, 0, "s")
+        turn_q(0, 2)
+        load_x(1, 1)
+        widen_x(1, 0, 0, "s")
+        make_gi(2)
+        inter_x(0, 0, 1)
+        widen_x(1, 0, 3, "s")
+        quant_g("r", 1)
+        widen_x(1, 1, 2, "s")
+        widen_x(1, 1, 0, "s")
+        quant_x(0, 0)
+        drain_q(0, 2, "s")
+        quant_g("i", 0)
+        drain_q(0, 1, "s")
+        make_k("r", 3)
+        widen_x(1, 1, 1, "s")
+        quant_g("i", 1)
+        make_u(0, 0)
+        make_u(0, 1)
+        inter_x(1, 0, 0)
+        make_k("i", 0)
+        inter_x(1, 0, 1)
+        load_q(1, 1)
+        widen_x(1, 1, 3, "s")
+        drain_k("i", 0, "s")
+        quant_q(1, 0)
+        drain_k("r", 3, "s")
+        make_u(0, 3)
+        make_k("r", 0)
+        make_k("r", 1)
+        quant_q(0, 0)
+        drain_k("r", 0, "s")
+        quant_x(1, 0)
+        make_u(0, 2)
+        inter_x(1, 1, 0)
+        inter_x(1, 1, 1)
+        make_k("r", 2)
+        drain_k("r", 1, "s")
+        drain_k("r", 2, "s")
+        make_k("i", 2)
+        make_f(0, 0, 0)
+        make_k("i", 3)
+        make_k("i", 1)
+        drain_k("i", 1, "s")
+        drain_k("i", 2, "s")
+        turn_q(1, 3)
+        quant_x(1, 1)
+        make_f(0, 0, 1)
+        make_f(0, 256, 2)
+        drain_k("i", 3, "s")
+        turn_q(1, 2)
+        make_u(1, 2)
+        quant_f(0, 0)
+        make_u(1, 1)
+        drain_q(1, 2, "s")
+        synth(0, 0, 256, 1)
+        synth(0, 0, 256, 0)
+        drain_q(1, 3, "s")
+        make_f(0, 256, 3)
+        quant_q(1, 1)
+        make_u(1, 3)
+        quant_f(0, 256)
+        store(0, 0, 256, 1, "s")
+        make_u(1, 0)
+        quant_q(0, 1)
+        synth(0, 256, 512, 0)
+        make_f(1, 256, 2)
+        store(0, 0, 256, 0, "s")
+        make_f(1, 384, 3)
+        synth(0, 256, 512, 1)
+        synth(0, 256, 512, 3)
+        store(0, 256, 512, 0, "s")
+        synth(0, 0, 256, 2)
+        store(0, 256, 512, 1, "s")
+        store(0, 256, 512, 3, "s")
+        quant_f(1, 256)
+        quant_f(1, 384)
+        synth(0, 256, 512, 2)
+        make_f(1, 0, 0)
+        synth(1, 256, 384, 1)
+        store(0, 0, 256, 2, "s")
+        store(0, 256, 512, 2, "s")
+        synth(0, 0, 256, 3)
+        synth(1, 384, 512, 1)
+        store(1, 256, 384, 1, "s")
+        store(0, 0, 256, 3, "s")
+        synth(1, 384, 512, 0)
+        make_f(1, 0, 1)
+        synth(1, 256, 384, 0)
+        store(1, 384, 512, 1, "s")
+        quant_f(1, 0)
+        store(1, 384, 512, 0, "s")
+        synth(1, 0, 256, 2)
+        store(1, 256, 384, 0, "v")
+        synth(1, 0, 256, 3)
+        store(1, 0, 256, 2, "v")
+        store(1, 0, 256, 3, "v")
+        synth(1, 0, 256, 1)
+        store(1, 0, 256, 1, "v")
+        synth(1, 0, 256, 0)
+        store(1, 0, 256, 0, "s")

@@ -210,7 +210,10 @@ def tile_cauchytransferfunctionfilter_w4_kernel(
 
         def inter_x(i, g, h):
             cols = slice(256 * h, 256 * (h + 1))
-            nc.vector.tensor_copy(out=inter[i, g][:, cols, :], in_=wide[i, g][:, :, cols].rearrange("p t d -> p d t"))
+            nc.vector.tensor_copy(
+                out=inter[i, g][:, cols, :].rearrange("p (c e) t -> p c t e", e=4),
+                in_=wide[i, g][:, :, cols].rearrange("p t (c e) -> p c t e", e=4),
+            )
 
         def quant_x(i, g):
             x_codes_t = keep.tile([P, D], U32, name="x_codes_%d_%d" % (i, g), align_bytes=64)
@@ -344,159 +347,159 @@ def tile_cauchytransferfunctionfilter_w4_kernel(
                 out=out[i].rearrange("(p j) d -> p j d", j=J)[:, tiles * jj : tiles * (jj + 1), d0:d1], in_=o_view
             )
 
-        load_x(0, 1)
-        load_vectors()
-        widen_x(0, 1, 3, "v")
-        make_de(0)
-        load_p()
-        widen_x(0, 1, 1, "s")
-        widen_x(0, 1, 2, "v")
-        widen_x(0, 1, 0, "s")
-        load_q(1, 0)
-        make_p(1)
-        make_de(1)
-        square(1)
-        load_q(0, 0)
-        load_p_scale()
-        make_p(0)
-        inter_x(0, 1, 0)
-        make_de(3)
-        inter_x(0, 1, 1)
-        turn_q(1, 1)
-        make_de(2)
-        square(0)
         load_x(0, 0)
-        make_p_scale(1)
-        make_r(0)
-        square(3)
-        make_p_scale(0)
-        load_q(0, 1)
-        make_w(0)
-        square(2)
-        load_c_scale()
-        quant_x(0, 1)
-        turn_q(0, 0)
-        make_r(1)
-        load_x(1, 0)
-        drain_q(1, 1, "s")
+        load_vectors()
+        widen_x(0, 0, 3, "s")
+        widen_x(0, 0, 1, "v")
         widen_x(0, 0, 2, "s")
-        widen_x(0, 0, 1, "s")
-        make_gr(0)
-        widen_x(1, 0, 1, "s")
+        load_p()
+        widen_x(0, 0, 0, "v")
+        load_x(0, 1)
+        load_p_scale()
+        make_de(1)
+        make_p(1)
+        widen_x(0, 1, 1, "s")
+        make_de(2)
+        widen_x(0, 1, 3, "s")
+        widen_x(0, 1, 0, "s")
+        make_de(0)
+        make_p(0)
+        inter_x(0, 0, 1)
+        make_de(3)
+        load_q(0, 0)
+        turn_q(0, 1)
+        widen_x(0, 1, 2, "s")
+        square(2)
+        inter_x(0, 0, 0)
+        turn_q(0, 0)
+        square(3)
+        square(1)
+        inter_x(0, 1, 1)
+        square(0)
+        quant_x(0, 0)
+        inter_x(0, 1, 0)
+        load_q(1, 0)
+        load_q(0, 1)
+        load_x(1, 0)
+        make_p_scale(0)
+        make_r(1)
+        make_r(0)
+        drain_q(0, 0, "s")
+        load_q(1, 1)
+        drain_q(0, 1, "s")
+        turn_q(1, 1)
+        widen_x(1, 0, 0, "s")
+        quant_x(0, 1)
+        turn_q(1, 0)
+        turn_q(1, 3)
+        make_p_scale(1)
         make_w(1)
         load_c()
-        make_gi(0)
-        widen_x(0, 0, 0, "s")
-        quant_g("r", 0)
-        turn_q(1, 0)
-        widen_x(0, 0, 3, "s")
-        make_gi(1)
-        turn_q(0, 3)
-        make_gr(1)
-        turn_q(0, 1)
-        drain_q(0, 0, "s")
-        widen_x(1, 0, 2, "s")
-        make_gi(3)
-        drain_q(0, 3, "s")
-        inter_x(0, 0, 0)
-        drain_q(1, 0, "s")
-        turn_q(0, 2)
-        load_x(1, 1)
-        widen_x(1, 0, 0, "s")
-        make_gi(2)
-        inter_x(0, 0, 1)
+        make_w(0)
+        turn_q(1, 2)
+        load_c_scale()
         widen_x(1, 0, 3, "s")
-        quant_g("r", 1)
-        widen_x(1, 1, 2, "s")
-        widen_x(1, 1, 0, "s")
-        quant_x(0, 0)
-        drain_q(0, 2, "s")
-        quant_g("i", 0)
-        drain_q(0, 1, "s")
-        make_k("r", 3)
-        widen_x(1, 1, 1, "s")
-        quant_g("i", 1)
-        make_u(0, 0)
+        load_x(1, 1)
+        drain_q(1, 1, "s")
+        quant_q(0, 0)
+        make_gi(0)
+        make_gi(1)
+        make_gi(2)
+        drain_q(1, 3, "s")
+        drain_q(1, 2, "s")
+        turn_q(0, 2)
         make_u(0, 1)
-        inter_x(1, 0, 0)
-        make_k("i", 0)
-        inter_x(1, 0, 1)
-        load_q(1, 1)
+        widen_x(1, 1, 0, "s")
+        widen_x(1, 1, 1, "s")
+        drain_q(1, 0, "s")
+        make_gr(1)
+        make_gi(3)
+        quant_g("r", 1)
+        widen_x(1, 0, 1, "s")
+        make_gr(0)
         widen_x(1, 1, 3, "s")
+        quant_g("i", 0)
+        quant_g("i", 1)
+        widen_x(1, 1, 2, "s")
+        quant_g("r", 0)
+        make_u(0, 0)
+        turn_q(0, 3)
+        make_u(0, 2)
+        make_k("i", 0)
+        widen_x(1, 0, 2, "s")
+        make_u(0, 3)
+        drain_q(0, 2, "s")
+        make_k("i", 1)
+        drain_q(0, 3, "s")
+        make_k("r", 1)
+        inter_x(1, 1, 0)
+        make_k("r", 2)
         drain_k("i", 0, "s")
+        make_k("i", 3)
+        drain_k("r", 1, "s")
+        drain_k("i", 1, "s")
+        inter_x(1, 0, 1)
+        inter_x(1, 0, 0)
+        make_k("r", 0)
+        inter_x(1, 1, 1)
+        make_k("r", 3)
+        drain_k("r", 2, "s")
+        quant_x(1, 0)
+        quant_x(1, 1)
+        drain_k("r", 0, "s")
+        make_k("i", 2)
+        make_f(0, 0, 1)
+        make_f(0, 0, 0)
+        quant_q(1, 1)
+        quant_f(0, 0)
+        drain_k("i", 2, "s")
+        make_u(1, 2)
+        drain_k("i", 3, "s")
+        make_u(1, 1)
+        quant_q(0, 1)
         quant_q(1, 0)
         drain_k("r", 3, "s")
-        make_u(0, 3)
-        make_k("r", 0)
-        make_k("r", 1)
-        quant_q(0, 0)
-        drain_k("r", 0, "s")
-        quant_x(1, 0)
-        make_u(0, 2)
-        inter_x(1, 1, 0)
-        inter_x(1, 1, 1)
-        make_k("r", 2)
-        drain_k("r", 1, "s")
-        drain_k("r", 2, "s")
-        make_k("i", 2)
-        make_f(0, 0, 0)
-        make_k("i", 3)
-        make_k("i", 1)
-        drain_k("i", 1, "s")
-        drain_k("i", 2, "s")
-        turn_q(1, 3)
-        quant_x(1, 1)
-        make_f(0, 0, 1)
-        make_f(0, 256, 2)
-        drain_k("i", 3, "s")
-        turn_q(1, 2)
-        make_u(1, 2)
-        quant_f(0, 0)
-        make_u(1, 1)
-        drain_q(1, 2, "s")
-        synth(0, 0, 256, 1)
-        synth(0, 0, 256, 0)
-        drain_q(1, 3, "s")
-        make_f(0, 256, 3)
-        quant_q(1, 1)
-        make_u(1, 3)
-        quant_f(0, 256)
-        store(0, 0, 256, 1, "s")
-        make_u(1, 0)
-        quant_q(0, 1)
-        synth(0, 256, 512, 0)
-        make_f(1, 256, 2)
-        store(0, 0, 256, 0, "s")
-        make_f(1, 384, 3)
-        synth(0, 256, 512, 1)
-        synth(0, 256, 512, 3)
-        store(0, 256, 512, 0, "s")
-        synth(0, 0, 256, 2)
-        store(0, 256, 512, 1, "s")
-        store(0, 256, 512, 3, "s")
-        quant_f(1, 256)
-        quant_f(1, 384)
-        synth(0, 256, 512, 2)
-        make_f(1, 0, 0)
-        synth(1, 256, 384, 1)
-        store(0, 0, 256, 2, "s")
-        store(0, 256, 512, 2, "s")
         synth(0, 0, 256, 3)
-        synth(1, 384, 512, 1)
-        store(1, 256, 384, 1, "s")
+        synth(0, 0, 256, 2)
+        make_f(0, 256, 3)
+        synth(0, 0, 256, 1)
         store(0, 0, 256, 3, "s")
-        synth(1, 384, 512, 0)
+        store(0, 0, 256, 2, "s")
+        make_f(0, 256, 2)
+        quant_f(0, 256)
+        synth(0, 0, 256, 0)
+        make_u(1, 3)
+        make_f(1, 384, 3)
+        store(0, 0, 256, 0, "s")
+        synth(0, 256, 512, 2)
+        make_f(1, 256, 2)
+        store(0, 0, 256, 1, "s")
+        store(0, 256, 512, 2, "s")
+        synth(0, 256, 512, 1)
+        synth(0, 256, 512, 0)
+        synth(0, 256, 512, 3)
+        quant_f(1, 384)
+        store(0, 256, 512, 1, "s")
+        store(0, 256, 512, 0, "s")
+        quant_f(1, 256)
+        make_u(1, 0)
+        store(0, 256, 512, 3, "s")
+        synth(1, 256, 384, 1)
         make_f(1, 0, 1)
+        make_f(1, 0, 0)
+        synth(1, 384, 512, 0)
+        store(1, 256, 384, 1, "s")
+        store(1, 384, 512, 0, "s")
+        synth(1, 384, 512, 1)
         synth(1, 256, 384, 0)
         store(1, 384, 512, 1, "s")
         quant_f(1, 0)
-        store(1, 384, 512, 0, "s")
+        store(1, 256, 384, 0, "s")
+        synth(1, 0, 256, 1)
         synth(1, 0, 256, 2)
-        store(1, 256, 384, 0, "v")
         synth(1, 0, 256, 3)
+        store(1, 0, 256, 1, "s")
         store(1, 0, 256, 2, "v")
         store(1, 0, 256, 3, "v")
-        synth(1, 0, 256, 1)
-        store(1, 0, 256, 1, "v")
         synth(1, 0, 256, 0)
         store(1, 0, 256, 0, "s")

@@ -274,6 +274,13 @@ def tile_cauchytransferfunctionfilter_w4_kernel(
                     stop=True,
                 )
 
+        def warm_pe(h):
+            bank = psum.tile([P, 512], F32, tag="a", name="warm_ps")
+            src = g_bf["r"][:].rearrange("p m t -> p (m t)")
+            for s in range(2):
+                cols = slice(1024 * h + 512 * s, 1024 * h + 512 * (s + 1))
+                nc.tensor.matmul(out=bank[:], lhsT=lhs_rows[:, 0:P], rhs=src[:, cols], start=True, stop=True)
+
         def drain_k(k, ch, engine):
             drain(k_sb[:, 0 if k == "r" else 1, ch, :, :], k_ps[k, ch][:].rearrange("p t d -> p d t"), engine)
 
@@ -347,159 +354,161 @@ def tile_cauchytransferfunctionfilter_w4_kernel(
                 out=out[i].rearrange("(p j) d -> p j d", j=J)[:, tiles * jj : tiles * (jj + 1), d0:d1], in_=o_view
             )
 
-        load_x(0, 0)
-        load_vectors()
-        widen_x(0, 0, 3, "s")
-        widen_x(0, 0, 1, "v")
-        widen_x(0, 0, 2, "s")
         load_p()
-        widen_x(0, 0, 0, "v")
         load_x(0, 1)
-        load_p_scale()
+        load_vectors()
         make_de(1)
-        make_p(1)
-        widen_x(0, 1, 1, "s")
-        make_de(2)
-        widen_x(0, 1, 3, "s")
-        widen_x(0, 1, 0, "s")
-        make_de(0)
-        make_p(0)
-        inter_x(0, 0, 1)
-        make_de(3)
-        load_q(0, 0)
-        turn_q(0, 1)
         widen_x(0, 1, 2, "s")
-        square(2)
-        inter_x(0, 0, 0)
-        turn_q(0, 0)
-        square(3)
-        square(1)
-        inter_x(0, 1, 1)
-        square(0)
-        quant_x(0, 0)
-        inter_x(0, 1, 0)
+        load_x(0, 0)
+        make_p(0)
         load_q(1, 0)
-        load_q(0, 1)
-        load_x(1, 0)
-        make_p_scale(0)
-        make_r(1)
-        make_r(0)
-        drain_q(0, 0, "s")
-        load_q(1, 1)
-        drain_q(0, 1, "s")
-        turn_q(1, 1)
-        widen_x(1, 0, 0, "s")
-        quant_x(0, 1)
+        widen_x(0, 1, 1, "s")
+        make_p(1)
+        make_de(3)
+        widen_x(0, 1, 3, "s")
+        make_de(0)
+        load_p_scale()
+        widen_x(0, 1, 0, "v")
+        load_q(0, 0)
+        widen_x(0, 0, 3, "v")
+        widen_x(0, 0, 2, "s")
+        make_de(2)
         turn_q(1, 0)
-        turn_q(1, 3)
-        make_p_scale(1)
-        make_w(1)
-        load_c()
+        inter_x(0, 1, 1)
+        widen_x(0, 0, 0, "s")
+        inter_x(0, 1, 0)
+        widen_x(0, 0, 1, "s")
+        inter_x(0, 0, 0)
+        square(1)
+        square(0)
+        inter_x(0, 0, 1)
+        make_r(0)
+        load_q(1, 1)
+        turn_q(0, 1)
+        load_x(1, 0)
+        square(3)
+        load_q(0, 1)
+        quant_x(0, 1)
+        quant_x(0, 0)
+        square(2)
+        make_p_scale(0)
         make_w(0)
-        turn_q(1, 2)
-        load_c_scale()
-        widen_x(1, 0, 3, "s")
-        load_x(1, 1)
-        drain_q(1, 1, "s")
-        quant_q(0, 0)
-        make_gi(0)
+        make_p_scale(1)
         make_gi(1)
-        make_gi(2)
-        drain_q(1, 3, "s")
-        drain_q(1, 2, "s")
-        turn_q(0, 2)
-        make_u(0, 1)
-        widen_x(1, 1, 0, "s")
-        widen_x(1, 1, 1, "s")
         drain_q(1, 0, "s")
-        make_gr(1)
-        make_gi(3)
-        quant_g("r", 1)
-        widen_x(1, 0, 1, "s")
-        make_gr(0)
-        widen_x(1, 1, 3, "s")
+        make_gi(0)
+        make_r(1)
+        make_w(1)
         quant_g("i", 0)
-        quant_g("i", 1)
-        widen_x(1, 1, 2, "s")
-        quant_g("r", 0)
-        make_u(0, 0)
-        turn_q(0, 3)
-        make_u(0, 2)
-        make_k("i", 0)
+        make_gr(0)
+        turn_q(1, 1)
+        widen_x(1, 0, 3, "s")
+        make_gi(3)
+        load_x(1, 1)
+        widen_x(1, 0, 1, "s")
+        make_gr(1)
+        drain_q(0, 1, "s")
+        drain_q(1, 1, "s")
+        widen_x(1, 0, 0, "s")
         widen_x(1, 0, 2, "s")
+        quant_g("r", 0)
+        load_c()
+        widen_x(1, 1, 1, "s")
+        load_c_scale()
+        turn_q(0, 0)
+        turn_q(0, 2)
         make_u(0, 3)
-        drain_q(0, 2, "s")
-        make_k("i", 1)
-        drain_q(0, 3, "s")
-        make_k("r", 1)
-        inter_x(1, 1, 0)
-        make_k("r", 2)
-        drain_k("i", 0, "s")
-        make_k("i", 3)
-        drain_k("r", 1, "s")
-        drain_k("i", 1, "s")
+        drain_q(0, 0, "s")
+        make_gi(2)
+        turn_q(1, 3)
         inter_x(1, 0, 1)
+        turn_q(1, 2)
         inter_x(1, 0, 0)
-        make_k("r", 0)
-        inter_x(1, 1, 1)
+        widen_x(1, 1, 3, "s")
+        widen_x(1, 1, 0, "s")
+        drain_q(0, 2, "s")
+        make_u(0, 2)
+        make_u(0, 1)
+        quant_g("i", 1)
+        drain_q(1, 3, "s")
+        make_u(0, 0)
+        drain_q(1, 2, "s")
+        widen_x(1, 1, 2, "s")
+        quant_g("r", 1)
+        warm_pe(1)
         make_k("r", 3)
-        drain_k("r", 2, "s")
-        quant_x(1, 0)
-        quant_x(1, 1)
-        drain_k("r", 0, "s")
-        make_k("i", 2)
-        make_f(0, 0, 1)
-        make_f(0, 0, 0)
-        quant_q(1, 1)
-        quant_f(0, 0)
-        drain_k("i", 2, "s")
-        make_u(1, 2)
-        drain_k("i", 3, "s")
-        make_u(1, 1)
-        quant_q(0, 1)
+        make_k("i", 3)
         quant_q(1, 0)
+        quant_x(1, 0)
+        inter_x(1, 1, 0)
         drain_k("r", 3, "s")
-        synth(0, 0, 256, 3)
-        synth(0, 0, 256, 2)
+        drain_k("i", 3, "s")
+        inter_x(1, 1, 1)
+        make_k("i", 2)
         make_f(0, 256, 3)
-        synth(0, 0, 256, 1)
-        store(0, 0, 256, 3, "s")
-        store(0, 0, 256, 2, "s")
+        make_k("r", 2)
+        drain_k("i", 2, "s")
+        make_k("i", 0)
+        quant_x(1, 1)
+        turn_q(0, 3)
+        drain_k("r", 2, "s")
+        drain_k("i", 0, "s")
         make_f(0, 256, 2)
-        quant_f(0, 256)
-        synth(0, 0, 256, 0)
+        make_k("i", 1)
+        make_k("r", 0)
+        quant_q(0, 0)
+        drain_q(0, 3, "s")
         make_u(1, 3)
-        make_f(1, 384, 3)
-        store(0, 0, 256, 0, "s")
-        synth(0, 256, 512, 2)
-        make_f(1, 256, 2)
-        store(0, 0, 256, 1, "s")
-        store(0, 256, 512, 2, "s")
+        quant_f(0, 256)
+        make_u(1, 1)
+        make_k("r", 1)
+        quant_q(0, 1)
+        drain_k("r", 0, "s")
+        drain_k("i", 1, "s")
+        quant_q(1, 1)
+        drain_k("r", 1, "s")
         synth(0, 256, 512, 1)
         synth(0, 256, 512, 0)
         synth(0, 256, 512, 3)
-        quant_f(1, 384)
-        store(0, 256, 512, 1, "s")
-        store(0, 256, 512, 0, "s")
-        quant_f(1, 256)
-        make_u(1, 0)
+        make_f(0, 0, 1)
+        synth(0, 256, 512, 2)
         store(0, 256, 512, 3, "s")
-        synth(1, 256, 384, 1)
-        make_f(1, 0, 1)
+        store(0, 256, 512, 0, "s")
+        store(0, 256, 512, 1, "s")
+        make_f(0, 0, 0)
+        make_u(1, 2)
+        store(0, 256, 512, 2, "s")
+        quant_f(0, 0)
+        make_u(1, 0)
+        synth(0, 0, 256, 3)
+        synth(0, 0, 256, 1)
+        synth(0, 0, 256, 0)
+        store(0, 0, 256, 3, "s")
+        make_f(1, 256, 2)
+        store(0, 0, 256, 1, "s")
+        make_f(1, 384, 3)
+        store(0, 0, 256, 0, "s")
+        quant_f(1, 256)
+        synth(0, 0, 256, 2)
+        quant_f(1, 384)
         make_f(1, 0, 0)
-        synth(1, 384, 512, 0)
-        store(1, 256, 384, 1, "s")
-        store(1, 384, 512, 0, "s")
-        synth(1, 384, 512, 1)
         synth(1, 256, 384, 0)
-        store(1, 384, 512, 1, "s")
-        quant_f(1, 0)
+        make_f(1, 0, 1)
+        synth(1, 384, 512, 0)
+        synth(1, 256, 384, 1)
+        store(0, 0, 256, 2, "s")
+        synth(1, 384, 512, 1)
         store(1, 256, 384, 0, "s")
-        synth(1, 0, 256, 1)
-        synth(1, 0, 256, 2)
+        store(1, 384, 512, 0, "s")
+        quant_f(1, 0)
+        store(1, 256, 384, 1, "s")
         synth(1, 0, 256, 3)
-        store(1, 0, 256, 1, "s")
-        store(1, 0, 256, 2, "v")
-        store(1, 0, 256, 3, "v")
+        synth(1, 0, 256, 1)
+        store(1, 384, 512, 1, "s")
+        synth(1, 0, 256, 2)
         synth(1, 0, 256, 0)
+        store(1, 0, 256, 3, "s")
+        store(1, 0, 256, 1, "s")
+        warm_pe(0)
+        store(1, 0, 256, 2, "v")
         store(1, 0, 256, 0, "s")

@@ -61,13 +61,14 @@ def tile_cauchytransferfunctionfilter_w4_kernel(
             nc.sync.dma_start(out=xs[:], in_=x_scale.rearrange("o (g p t) w -> p (o g) (t w)", p=P, t=T))
             nc.sync.dma_start(out=b_col[:], in_=b.rearrange("(p t) -> p t", t=T))
 
-        def load_x(i, g):
-            x_raw_t = keep.tile([P, T * D], U8, name="x_raw_%d_%d" % (i, g))
-            nc.sync.dma_start(
-                out=x_raw_t[:],
-                in_=x_bytes[i, g * 512 : (g + 1) * 512, :].rearrange("(p t) d -> p (t d)", t=T),
-            )
-            x_raw[i, g] = x_raw_t
+        for i in range(B):
+            for g in range(G):
+                x_raw_t = keep.tile([P, T * D], U8, name="x_raw_%d_%d" % (i, g))
+                x_raw[i, g] = x_raw_t
+
+        def load_x(i, g, t0, t1):
+            rows = x_bytes[i, g * 512 : (g + 1) * 512, :].rearrange("(p t) d -> p (t d)", t=T)
+            nc.sync.dma_start(out=x_raw[i, g][:, t0 * D : t1 * D], in_=rows[:, t0 * D : t1 * D])
 
         def load_p():
             nc.sync.dma_start(out=p_raw[:], in_=p_words.rearrange("g p w -> p g w"))
@@ -143,8 +144,8 @@ def tile_cauchytransferfunctionfilter_w4_kernel(
 
         def make_gr(h):
             cols = slice(256 * h, 256 * (h + 1))
-            nc.vector.tensor_scalar(
-                out=g_bf["r"][:, cols, :], in0=w_mt[:, cols, :], scalar1=0.5, scalar2=None, op0=ALU.mult
+            nc.gpsimd.tensor_scalar(
+                out=g_bf["r"][:, cols, :], in0=w_mt[:, cols, :], scalar1=0.5, scalar2=0.0, op0=ALU.mult, op1=ALU.add
             )
 
         def make_gi(tm):
@@ -354,161 +355,162 @@ def tile_cauchytransferfunctionfilter_w4_kernel(
                 out=out[i].rearrange("(p j) d -> p j d", j=J)[:, tiles * jj : tiles * (jj + 1), d0:d1], in_=o_view
             )
 
-        load_p()
-        load_x(0, 1)
+        load_x(1, 1, 0, 4)
         load_vectors()
-        make_de(1)
-        widen_x(0, 1, 2, "s")
-        load_x(0, 0)
-        make_p(0)
-        load_q(1, 0)
-        widen_x(0, 1, 1, "s")
-        make_p(1)
-        make_de(3)
-        widen_x(0, 1, 3, "s")
         make_de(0)
+        widen_x(1, 1, 1, "v")
+        make_de(1)
+        load_p()
+        load_x(0, 1, 0, 4)
+        widen_x(1, 1, 3, "s")
+        widen_x(1, 1, 0, "v")
+        make_de(2)
+        widen_x(1, 1, 2, "s")
+        load_q(0, 0)
+        make_p(0)
+        make_de(3)
+        widen_x(0, 1, 2, "s")
+        inter_x(1, 1, 0)
+        widen_x(0, 1, 3, "s")
+        widen_x(0, 1, 1, "s")
+        square(0)
+        load_q(1, 1)
+        square(1)
         load_p_scale()
         widen_x(0, 1, 0, "v")
-        load_q(0, 0)
-        widen_x(0, 0, 3, "v")
-        widen_x(0, 0, 2, "s")
-        make_de(2)
-        turn_q(1, 0)
-        inter_x(0, 1, 1)
-        widen_x(0, 0, 0, "s")
-        inter_x(0, 1, 0)
-        widen_x(0, 0, 1, "s")
-        inter_x(0, 0, 0)
-        square(1)
-        square(0)
-        inter_x(0, 0, 1)
-        make_r(0)
-        load_q(1, 1)
-        turn_q(0, 1)
-        load_x(1, 0)
         square(3)
-        load_q(0, 1)
-        quant_x(0, 1)
-        quant_x(0, 0)
+        make_r(0)
+        make_p(1)
         square(2)
-        make_p_scale(0)
+        inter_x(1, 1, 1)
+        inter_x(0, 1, 0)
+        load_x(0, 0, 2, 4)
+        turn_q(0, 0)
+        turn_q(1, 3)
+        drain_q(0, 0, "s")
+        load_x(0, 0, 0, 2)
+        inter_x(0, 1, 1)
+        drain_q(1, 3, "s")
+        quant_x(1, 1)
         make_w(0)
-        make_p_scale(1)
-        make_gi(1)
-        drain_q(1, 0, "s")
+        turn_q(1, 2)
+        load_q(1, 0)
+        make_p_scale(0)
+        make_gr(0)
         make_gi(0)
         make_r(1)
+        drain_q(1, 2, "s")
+        make_gi(1)
+        turn_q(0, 1)
         make_w(1)
+        turn_q(1, 0)
+        widen_x(0, 0, 3, "s")
         quant_g("i", 0)
-        make_gr(0)
-        turn_q(1, 1)
-        widen_x(1, 0, 3, "s")
-        make_gi(3)
-        load_x(1, 1)
-        widen_x(1, 0, 1, "s")
-        make_gr(1)
+        load_q(0, 1)
+        make_gi(2)
+        turn_q(0, 3)
         drain_q(0, 1, "s")
+        widen_x(0, 0, 0, "s")
+        widen_x(0, 0, 1, "s")
+        drain_q(1, 0, "s")
+        turn_q(1, 1)
+        widen_x(0, 0, 2, "s")
+        turn_q(0, 2)
+        drain_q(0, 3, "s")
+        load_x(1, 0, 0, 4)
         drain_q(1, 1, "s")
-        widen_x(1, 0, 0, "s")
+        make_gi(3)
+        make_gr(1)
+        warm_pe(0)
+        drain_q(0, 2, "s")
         widen_x(1, 0, 2, "s")
         quant_g("r", 0)
         load_c()
-        widen_x(1, 1, 1, "s")
-        load_c_scale()
-        turn_q(0, 0)
-        turn_q(0, 2)
-        make_u(0, 3)
-        drain_q(0, 0, "s")
-        make_gi(2)
-        turn_q(1, 3)
-        inter_x(1, 0, 1)
-        turn_q(1, 2)
-        inter_x(1, 0, 0)
-        widen_x(1, 1, 3, "s")
-        widen_x(1, 1, 0, "s")
-        drain_q(0, 2, "s")
-        make_u(0, 2)
-        make_u(0, 1)
+        widen_x(1, 0, 1, "s")
         quant_g("i", 1)
-        drain_q(1, 3, "s")
-        make_u(0, 0)
-        drain_q(1, 2, "s")
-        widen_x(1, 1, 2, "s")
-        quant_g("r", 1)
+        widen_x(1, 0, 0, "s")
+        widen_x(1, 0, 3, "s")
         warm_pe(1)
-        make_k("r", 3)
-        make_k("i", 3)
-        quant_q(1, 0)
-        quant_x(1, 0)
-        inter_x(1, 1, 0)
-        drain_k("r", 3, "s")
-        drain_k("i", 3, "s")
-        inter_x(1, 1, 1)
-        make_k("i", 2)
-        make_f(0, 256, 3)
-        make_k("r", 2)
-        drain_k("i", 2, "s")
-        make_k("i", 0)
-        quant_x(1, 1)
-        turn_q(0, 3)
-        drain_k("r", 2, "s")
-        drain_k("i", 0, "s")
-        make_f(0, 256, 2)
+        quant_g("r", 1)
+        inter_x(0, 0, 1)
+        load_c_scale()
         make_k("i", 1)
-        make_k("r", 0)
-        quant_q(0, 0)
-        drain_q(0, 3, "s")
-        make_u(1, 3)
-        quant_f(0, 256)
-        make_u(1, 1)
-        make_k("r", 1)
-        quant_q(0, 1)
-        drain_k("r", 0, "s")
         drain_k("i", 1, "s")
-        quant_q(1, 1)
+        inter_x(0, 0, 0)
+        make_k("r", 0)
+        make_p_scale(1)
+        quant_x(0, 0)
+        quant_x(0, 1)
+        make_k("i", 0)
+        drain_k("r", 0, "s")
+        make_k("r", 1)
+        make_u(0, 1)
+        quant_q(0, 1)
+        inter_x(1, 0, 0)
+        make_u(0, 0)
+        make_k("i", 2)
+        make_k("r", 3)
+        drain_k("i", 0, "s")
+        inter_x(1, 0, 1)
         drain_k("r", 1, "s")
-        synth(0, 256, 512, 1)
-        synth(0, 256, 512, 0)
-        synth(0, 256, 512, 3)
+        quant_q(0, 0)
+        quant_x(1, 0)
+        make_k("r", 2)
+        make_k("i", 3)
         make_f(0, 0, 1)
-        synth(0, 256, 512, 2)
-        store(0, 256, 512, 3, "s")
-        store(0, 256, 512, 0, "s")
-        store(0, 256, 512, 1, "s")
+        make_u(1, 3)
+        make_u(1, 1)
         make_f(0, 0, 0)
-        make_u(1, 2)
-        store(0, 256, 512, 2, "s")
+        quant_q(1, 1)
+        drain_k("r", 3, "s")
+        make_u(0, 2)
         quant_f(0, 0)
+        quant_q(1, 0)
         make_u(1, 0)
-        synth(0, 0, 256, 3)
-        synth(0, 0, 256, 1)
-        synth(0, 0, 256, 0)
-        store(0, 0, 256, 3, "s")
-        make_f(1, 256, 2)
-        store(0, 0, 256, 1, "s")
-        make_f(1, 384, 3)
-        store(0, 0, 256, 0, "s")
-        quant_f(1, 256)
+        drain_k("i", 3, "s")
+        drain_k("i", 2, "s")
         synth(0, 0, 256, 2)
-        quant_f(1, 384)
+        make_f(1, 384, 3)
+        drain_k("r", 2, "s")
         make_f(1, 0, 0)
-        synth(1, 256, 384, 0)
+        synth(0, 0, 256, 1)
+        quant_f(1, 384)
         make_f(1, 0, 1)
-        synth(1, 384, 512, 0)
-        synth(1, 256, 384, 1)
-        store(0, 0, 256, 2, "s")
-        synth(1, 384, 512, 1)
-        store(1, 256, 384, 0, "s")
-        store(1, 384, 512, 0, "s")
         quant_f(1, 0)
-        store(1, 256, 384, 1, "s")
-        synth(1, 0, 256, 3)
+        synth(0, 0, 256, 0)
+        store(0, 0, 256, 2, "s")
+        store(0, 0, 256, 0, "s")
+        store(0, 0, 256, 1, "s")
+        synth(0, 0, 256, 3)
+        make_u(0, 3)
+        synth(1, 384, 512, 0)
+        synth(1, 384, 512, 1)
+        store(0, 0, 256, 3, "s")
+        make_f(0, 256, 3)
+        make_f(0, 256, 2)
         synth(1, 0, 256, 1)
-        store(1, 384, 512, 1, "s")
         synth(1, 0, 256, 2)
+        quant_f(0, 256)
+        store(1, 384, 512, 0, "s")
+        store(1, 384, 512, 1, "s")
         synth(1, 0, 256, 0)
-        store(1, 0, 256, 3, "s")
         store(1, 0, 256, 1, "s")
-        warm_pe(0)
-        store(1, 0, 256, 2, "v")
+        synth(1, 0, 256, 3)
+        make_u(1, 2)
+        store(1, 0, 256, 2, "s")
+        synth(0, 256, 512, 3)
         store(1, 0, 256, 0, "s")
+        store(1, 0, 256, 3, "s")
+        make_f(1, 256, 2)
+        store(0, 256, 512, 3, "s")
+        synth(0, 256, 512, 0)
+        quant_f(1, 256)
+        synth(0, 256, 512, 1)
+        store(0, 256, 512, 0, "s")
+        synth(0, 256, 512, 2)
+        store(0, 256, 512, 1, "s")
+        store(0, 256, 512, 2, "s")
+        synth(1, 256, 384, 0)
+        synth(1, 256, 384, 1)
+        store(1, 256, 384, 0, "s")
+        store(1, 256, 384, 1, "s")

from contextlib import ExitStack

import concourse.mybir as mybir
from concourse.masks import make_identity

B, S, D, M, N, C = 2, 1024, 512, 512, 512, 2
FLOPS = 2 * (2 * M * N * D + B * M * S * D + 2 * B * S * M * D)

F32 = mybir.dt.float32
BF16 = mybir.dt.bfloat16
U32 = mybir.dt.uint32
I32 = mybir.dt.int32
U8 = mybir.dt.uint8
F8 = mybir.dt.float8_e4m3fn
E4M3 = mybir.dt.float8_e4m3fn_x4
E2M1 = mybir.dt.float4_e2m1fn_x4
ALU = mybir.AluOpType
ACT = mybir.ActivationFunctionType

P = 128
T = 4
G = S // 512
CH = D // P
J = S // P
UNITS = [[(0, 256), (256, 512)], [(0, 256), (256, 384), (384, 512)]]


def tile_cauchytransferfunctionfilter_w4_kernel(
    tc, x_bytes, x_scale, p_words, p_scales, om, nu, b, c_words, c_scales, q, out
):
    nc = tc.nc
    with ExitStack() as ctx:
        keep = ctx.enter_context(tc.tile_pool(name="keep", bufs=1))
        outp = ctx.enter_context(tc.tile_pool(name="outp", bufs=6))
        psum = ctx.enter_context(tc.psum_pool(name="psum", bufs=4))

        lhs_rows = keep.tile([P, N], BF16)
        rhs_rows = keep.tile([P, M], BF16)
        quarter = keep.tile([P, 1], F32)
        warm = keep.tile([P, 1], F32)
        p_scale_raw = keep.tile([P, G, M], U8, align_bytes=64)
        c_scale = keep.tile([P, D], U8, align_bytes=64)
        nc.vector.memset(rhs_rows[:].bitcast(F32), 0.0)
        nc.gpsimd.memset(lhs_rows[:].bitcast(F32), 0.0)
        nc.vector.memset(quarter[:], 0.25)
        nc.vector.memset(rhs_rows[32:33, :], -1.0)
        nc.vector.memset(lhs_rows[0:1, :], 1.0)
        nc.scalar.activation(out=warm[:], in_=quarter[:], func=ACT.Abs_reciprocal_sqrt, bias=quarter[:], scale=1.0)
        nc.vector.memset(p_scale_raw[:].rearrange("p g m -> p (g m)").bitcast(I32), 0)
        nc.vector.memset(c_scale[:].bitcast(I32), 0)
        b_col = keep.tile([P, T], BF16)
        xs = keep.tile([P, G, T], F32)
        p_raw = keep.tile([P, G, 2 * M], U8, align_bytes=64)
        c_raw = keep.tile([P, 2 * D], U8, align_bytes=64)
        q_raw = keep.tile([P, C, J, M], BF16, align_bytes=64)
        x_raw = {}

        def load_vectors():
            nc.sync.dma_start(out=rhs_rows[0:1, :], in_=om.rearrange("(o m) -> o m", o=1))
            nc.sync.dma_start(out=lhs_rows[32:33, :], in_=nu.rearrange("(o n) -> o n", o=1))
            nc.sync.dma_start(out=xs[:], in_=x_scale.rearrange("o (g p t) w -> p (o g) (t w)", p=P, t=T))
            nc.sync.dma_start(out=b_col[:], in_=b.rearrange("(p t) -> p t", t=T))

        for i in range(B):
            for g in range(G):
                x_raw_t = keep.tile([P, T * D], U8, name="x_raw_%d_%d" % (i, g))
                x_raw[i, g] = x_raw_t

        def load_x(i, g, t0, t1):
            rows = x_bytes[i, g * 512 : (g + 1) * 512, :].rearrange("(p t) d -> p (t d)", t=T)
            nc.sync.dma_start(out=x_raw[i, g][:, t0 * D : t1 * D], in_=rows[:, t0 * D : t1 * D])

        def load_p():
            nc.sync.dma_start(out=p_raw[:], in_=p_words.rearrange("g p w -> p g w"))

        def load_p_scale():
            for r4 in range(4):
                nc.sync.dma_start(
                    out=p_scale_raw[32 * r4 : 32 * r4 + 4, :, :].bitcast(I32),
                    in_=p_scales[:, 4 * r4 : 4 * r4 + 4, :].rearrange("g q m -> q g m").bitcast(I32),
                )

        def load_c():
            nc.sync.dma_start(out=c_raw[:], in_=c_words[0])

        def load_c_scale():
            for r4 in range(4):
                nc.sync.dma_start(
                    out=c_scale[32 * r4 : 32 * r4 + 4, :].bitcast(I32),
                    in_=c_scales[0, 4 * r4 : 4 * r4 + 4, :].bitcast(I32),
                )

        def load_q(c, h):
            nc.sync.dma_start(
                out=q_raw[:, c, 4 * h : 4 * h + 4, :],
                in_=q[c].rearrange("(p j) m -> p j m", j=J)[:, 4 * h : 4 * h + 4, :],
            )

        ident = keep.tile([P, P], F32)
        make_identity(nc, ident[:])

        ctx.enter_context(tc.manual_schedule())
        r = keep.tile([P, T, M], F32)
        w = keep.tile([P, T, M], F32)
        de = {}

        def make_de(tm):
            de_ps = psum.tile([P, T, P], F32, tag="u")
            de[tm] = de_ps
            for t in range(T):
                nc.tensor.matmul(
                    out=de_ps[:, t, :], lhsT=lhs_rows[:, t::T], rhs=rhs_rows[:, tm::T], start=True, stop=True
                )

        def square(tm):
            nc.scalar.activation(out=r[:, :, P * tm : P * (tm + 1)], in_=de[tm][:], func=ACT.Square)

        def make_r(h):
            cols = slice(256 * h, 256 * (h + 1))
            nc.scalar.activation(
                out=r[:, :, cols], in_=r[:, :, cols], func=ACT.Abs_reciprocal_sqrt, bias=quarter[:], scale=1.0
            )

        def make_w(h):
            cols = slice(256 * h, 256 * (h + 1))
            for t in range(T):
                nc.vector.scalar_tensor_tensor(
                    out=w[:, t, cols],
                    in0=r[:, t, cols],
                    scalar=b_col[:, t : t + 1],
                    in1=r[:, t, cols],
                    op0=ALU.mult,
                    op1=ALU.mult,
                )

        g_bf, g_codes, g_scale = {}, {}, {}
        for k in ("r", "i"):
            g_bf_t = keep.tile([P, M, T], BF16, name="g_bf_" + k, align_bytes=64)
            g_codes_t = keep.tile([P, M], U32, name="g_codes_" + k, align_bytes=64)
            g_scale_t = keep.tile([P, M], U8, name="g_scale_" + k, align_bytes=64)
            g_bf[k], g_codes[k], g_scale[k] = g_bf_t, g_codes_t, g_scale_t

        w_mt = w[:].rearrange("p t m -> p m t")

        def make_gr(h):
            cols = slice(256 * h, 256 * (h + 1))
            nc.gpsimd.tensor_scalar(
                out=g_bf["r"][:, cols, :], in0=w_mt[:, cols, :], scalar1=0.5, scalar2=0.0, op0=ALU.mult, op1=ALU.add
            )

        def make_gi(tm):
            sub = slice(P * tm, P * (tm + 1))
            nc.vector.tensor_tensor(
                out=g_bf["i"][:, sub, :],
                in0=de[tm][:].rearrange("p t m -> p m t"),
                in1=w_mt[:, sub, :],
                op=ALU.mult,
            )

        def quant_g(k, h):
            cols = slice(256 * h, 256 * (h + 1))
            nc.vector.quantize_mx(
                out=g_codes[k][:, cols].bitcast(E4M3),
                scales=g_scale[k][:, cols],
                in_=g_bf[k][:, cols, :].rearrange("p m t -> p (m t)"),
            )

        p_perm = keep.tile([P, G, 2 * M], U8, align_bytes=64)
        p_scale = keep.tile([P, G, M], U8, align_bytes=64)

        def make_p(g):
            nc.vector.tensor_copy(
                out=p_perm[:, g, :].rearrange("p (t m e) -> p t m e", t=T, e=2),
                in_=p_raw[:, g, :].rearrange("p (m t e) -> p t m e", t=T, e=2),
            )

        def make_p_scale(g):
            nc.vector.tensor_copy(
                out=p_scale[:, g, :].rearrange("p (t m) -> p t m", t=T),
                in_=p_scale_raw[:, g, :].rearrange("p (m t) -> p t m", t=T),
            )

        x_codes, x_sc = {}, {}

        wide, inter = {}, {}

        for i in range(B):
            for g in range(G):
                wide_t = keep.tile([P, T, D], BF16, name="wide_%d_%d" % (i, g), align_bytes=64)
                wide[i, g] = wide_t

        def widen_x(i, g, t, engine):
            src = x_raw[i, g][:, t * D : (t + 1) * D].bitcast(F8)
            scale = xs[:, g, t : t + 1]
            dst = wide[i, g][:, t, :]
            if engine == "v":
                nc.vector.tensor_scalar(out=dst, in0=src, scalar1=scale, scalar2=None, op0=ALU.mult)
            else:
                nc.scalar.activation(out=dst, in_=src, func=ACT.Copy, scale=scale)

        def drain(out_view, in_view, engine):
            if engine == "v":
                nc.vector.tensor_copy(out=out_view, in_=in_view)
            else:
                nc.scalar.copy(out=out_view, in_=in_view)

        for i in range(B):
            for g in range(G):
                inter_t = keep.tile([P, D, T], BF16, name="inter_%d_%d" % (i, g), align_bytes=64)
                inter[i, g] = inter_t

        def inter_x(i, g, h):
            cols = slice(256 * h, 256 * (h + 1))
            nc.vector.tensor_copy(
                out=inter[i, g][:, cols, :].rearrange("p (c e) t -> p c t e", e=4),
                in_=wide[i, g][:, :, cols].rearrange("p t (c e) -> p c t e", e=4),
            )

        def quant_x(i, g):
            x_codes_t = keep.tile([P, D], U32, name="x_codes_%d_%d" % (i, g), align_bytes=64)
            x_sc_t = keep.tile([P, D], U8, name="x_sc_%d_%d" % (i, g), align_bytes=64)
            nc.vector.quantize_mx(
                out=x_codes_t[:].bitcast(E4M3), scales=x_sc_t[:], in_=inter[i, g][:].rearrange("p d t -> p (d t)")
            )
            x_codes[i, g], x_sc[i, g] = x_codes_t, x_sc_t

        q_codes = keep.tile([P, C, S], U32, align_bytes=64)
        q_sc = keep.tile([P, C, S], U8, align_bytes=64)
        q_bf = keep.tile([P, C, S, T], BF16, align_bytes=64)

        q_ps = {}

        def turn_q(c, jj):
            bank = psum.tile([P, 2, 2, P], F32, tag="a", name="q_ps")
            q_ps[c, jj] = bank
            words = q_raw[:, c, :, :].rearrange("p j m -> p (j m)").bitcast(F32)
            for k in range(2):
                for u in range(2):
                    base = (2 * jj + k) * (M // 2)
                    nc.tensor.transpose(bank[:, k, u, :], words[:, base + u : base + M // 2 : 2], ident[:])

        def drain_q(c, jj, engine):
            drain(
                q_bf[:, c, 2 * jj * P : (2 * jj + 2) * P, :]
                .rearrange("p s t -> p (s t)")
                .bitcast(F32)
                .rearrange("p (k s u) -> p k s u", k=2, u=2),
                q_ps[c, jj][:].rearrange("p k u s -> p k s u"),
                engine,
            )

        def quant_q(c, h):
            rows = slice(h * 512, (h + 1) * 512)
            nc.vector.quantize_mx(
                out=q_codes[:, c, rows].bitcast(E4M3),
                scales=q_sc[:, c, rows],
                in_=q_bf[:, c, rows, :].rearrange("p s t -> p (s t)"),
            )

        k_sb = keep.tile([P, 2, CH, P, T], F32)
        k_ps = {}

        def make_k(k, ch):
            bank = psum.tile([P, T, P], F32, tag="a", name="k_ps")
            k_ps[k, ch] = bank
            for t in range(T):
                cols = slice(t * P, (t + 1) * P)
                nc.tensor.matmul_mx(
                    out=bank[:, t, :],
                    lhsT=g_codes[k][:, cols].bitcast(E4M3),
                    lhsT_scale=g_scale[k][:, cols],
                    rhs=c_raw[:, 2 * P * ch : 2 * P * (ch + 1)].bitcast(E2M1),
                    rhs_scale=c_scale[:, P * ch : P * (ch + 1)],
                    start=True,
                    stop=True,
                )

        def warm_pe(h):
            bank = psum.tile([P, 512], F32, tag="a", name="warm_ps")
            src = g_bf["r"][:].rearrange("p m t -> p (m t)")
            for s in range(2):
                cols = slice(1024 * h + 512 * s, 1024 * h + 512 * (s + 1))
                nc.tensor.matmul(out=bank[:], lhsT=lhs_rows[:, 0:P], rhs=src[:, cols], start=True, stop=True)

        def drain_k(k, ch, engine):
            drain(k_sb[:, 0 if k == "r" else 1, ch, :, :], k_ps[k, ch][:].rearrange("p t d -> p d t"), engine)

        f_bf, f_codes, f_sc = {}, {}, {}
        for i in range(B):
            for d0, d1 in UNITS[i]:
                f_bf_t = keep.tile([P, 2, d1 - d0, T], BF16, name="f_bf_%d_%d" % (i, d0), align_bytes=64)
                f_codes_t = keep.tile([P, 2, d1 - d0], U32, name="f_codes_%d_%d" % (i, d0), align_bytes=64)
                f_sc_t = keep.tile([P, 2, d1 - d0], U8, name="f_sc_%d_%d" % (i, d0), align_bytes=64)
                f_bf[i, d0], f_codes[i, d0], f_sc[i, d0] = f_bf_t, f_codes_t, f_sc_t
        u_ps = {}

        def make_u(i, ch):
            bank = psum.tile([P, T, P], F32, tag="u", name="u_ps")
            u_ps[i, ch] = bank
            for t in range(T):
                for g in range(G):
                    nc.tensor.matmul_mx(
                        out=bank[:, t, :],
                        lhsT=p_perm[:, g, 2 * P * t : 2 * P * (t + 1)].bitcast(E2M1),
                        lhsT_scale=p_scale[:, g, P * t : P * (t + 1)],
                        rhs=x_codes[i, g][:, P * ch : P * (ch + 1)].bitcast(E4M3),
                        rhs_scale=x_sc[i, g][:, P * ch : P * (ch + 1)],
                        start=(g == 0),
                        stop=(g == G - 1),
                    )

        def make_f(i, d0, ch):
            nc.vector.tensor_tensor(
                out=f_bf[i, d0][:, :, P * ch - d0 : P * (ch + 1) - d0, :],
                in0=u_ps[i, ch][:].rearrange("p (o t) d -> p o d t", o=1).to_broadcast([P, 2, P, T]),
                in1=k_sb[:, :, ch, :, :],
                op=ALU.mult,
            )

        def quant_f(i, d0):
            nc.vector.quantize_mx(
                out=f_codes[i, d0][:].rearrange("p k d -> p (k d)").bitcast(E4M3),
                scales=f_sc[i, d0][:].rearrange("p k d -> p (k d)"),
                in_=f_bf[i, d0][:].rearrange("p k d t -> p (k d t)"),
            )

        o_ps = {}

        def synth(i, d0, d1, jj):
            width = d1 - d0
            tiles = 512 // width
            bank = psum.tile([P, tiles, width], F32, tag="a", name="o_ps")
            for kk in range(tiles):
                j = tiles * jj + kk
                for c in range(C):
                    cols = slice(j * P, (j + 1) * P)
                    nc.tensor.matmul_mx(
                        out=bank[:, kk, :],
                        lhsT=q_codes[:, c, cols].bitcast(E4M3),
                        lhsT_scale=q_sc[:, c, cols],
                        rhs=f_codes[i, d0][:, c, :].bitcast(E4M3),
                        rhs_scale=f_sc[i, d0][:, c, :],
                        start=(c == 0),
                        stop=(c == C - 1),
                    )
            o_ps[i, d0, jj] = bank

        def store(i, d0, d1, jj, engine):
            tiles = 512 // (d1 - d0)
            bank = o_ps[i, d0, jj]
            o_sb = outp.tile([P, 512], F32)
            o_view = o_sb[:].rearrange("p (k d) -> p k d", k=tiles)
            drain(o_view, bank[:], engine)
            nc.sync.dma_start(
                out=out[i].rearrange("(p j) d -> p j d", j=J)[:, tiles * jj : tiles * (jj + 1), d0:d1], in_=o_view
            )

        load_x(1, 1, 0, 4)
        load_vectors()
        make_de(0)
        widen_x(1, 1, 1, "v")
        make_de(1)
        load_p()
        load_x(0, 1, 0, 4)
        widen_x(1, 1, 3, "s")
        widen_x(1, 1, 0, "v")
        make_de(2)
        widen_x(1, 1, 2, "s")
        load_q(0, 0)
        make_p(0)
        make_de(3)
        widen_x(0, 1, 2, "s")
        inter_x(1, 1, 0)
        widen_x(0, 1, 3, "s")
        widen_x(0, 1, 1, "s")
        square(0)
        load_q(1, 1)
        square(1)
        load_p_scale()
        widen_x(0, 1, 0, "v")
        square(3)
        make_r(0)
        make_p(1)
        square(2)
        inter_x(1, 1, 1)
        inter_x(0, 1, 0)
        load_x(0, 0, 2, 4)
        turn_q(0, 0)
        turn_q(1, 3)
        drain_q(0, 0, "s")
        load_x(0, 0, 0, 2)
        inter_x(0, 1, 1)
        drain_q(1, 3, "s")
        quant_x(1, 1)
        make_w(0)
        turn_q(1, 2)
        load_q(1, 0)
        make_p_scale(0)
        make_gr(0)
        make_gi(0)
        make_r(1)
        drain_q(1, 2, "s")
        make_gi(1)
        turn_q(0, 1)
        make_w(1)
        turn_q(1, 0)
        widen_x(0, 0, 3, "s")
        quant_g("i", 0)
        load_q(0, 1)
        make_gi(2)
        turn_q(0, 3)
        drain_q(0, 1, "s")
        widen_x(0, 0, 0, "s")
        widen_x(0, 0, 1, "s")
        drain_q(1, 0, "s")
        turn_q(1, 1)
        widen_x(0, 0, 2, "s")
        turn_q(0, 2)
        drain_q(0, 3, "s")
        load_x(1, 0, 0, 4)
        drain_q(1, 1, "s")
        make_gi(3)
        make_gr(1)
        warm_pe(0)
        drain_q(0, 2, "s")
        widen_x(1, 0, 2, "s")
        quant_g("r", 0)
        load_c()
        widen_x(1, 0, 1, "s")
        quant_g("i", 1)
        widen_x(1, 0, 0, "s")
        widen_x(1, 0, 3, "s")
        warm_pe(1)
        quant_g("r", 1)
        inter_x(0, 0, 1)
        load_c_scale()
        make_k("i", 1)
        drain_k("i", 1, "s")
        inter_x(0, 0, 0)
        make_k("r", 0)
        make_p_scale(1)
        quant_x(0, 0)
        quant_x(0, 1)
        make_k("i", 0)
        drain_k("r", 0, "s")
        make_k("r", 1)
        make_u(0, 1)
        quant_q(0, 1)
        inter_x(1, 0, 0)
        make_u(0, 0)
        make_k("i", 2)
        make_k("r", 3)
        drain_k("i", 0, "s")
        inter_x(1, 0, 1)
        drain_k("r", 1, "s")
        quant_q(0, 0)
        quant_x(1, 0)
        make_k("r", 2)
        make_k("i", 3)
        make_f(0, 0, 1)
        make_u(1, 3)
        make_u(1, 1)
        make_f(0, 0, 0)
        quant_q(1, 1)
        drain_k("r", 3, "s")
        make_u(0, 2)
        quant_f(0, 0)
        quant_q(1, 0)
        make_u(1, 0)
        drain_k("i", 3, "s")
        drain_k("i", 2, "s")
        synth(0, 0, 256, 2)
        make_f(1, 384, 3)
        drain_k("r", 2, "s")
        make_f(1, 0, 0)
        synth(0, 0, 256, 1)
        quant_f(1, 384)
        make_f(1, 0, 1)
        quant_f(1, 0)
        synth(0, 0, 256, 0)
        store(0, 0, 256, 2, "s")
        store(0, 0, 256, 0, "s")
        store(0, 0, 256, 1, "s")
        synth(0, 0, 256, 3)
        make_u(0, 3)
        synth(1, 384, 512, 0)
        synth(1, 384, 512, 1)
        store(0, 0, 256, 3, "s")
        make_f(0, 256, 3)
        make_f(0, 256, 2)
        synth(1, 0, 256, 1)
        synth(1, 0, 256, 2)
        quant_f(0, 256)
        store(1, 384, 512, 0, "s")
        store(1, 384, 512, 1, "s")
        synth(1, 0, 256, 0)
        store(1, 0, 256, 1, "s")
        synth(1, 0, 256, 3)
        make_u(1, 2)
        store(1, 0, 256, 2, "s")
        synth(0, 256, 512, 3)
        store(1, 0, 256, 0, "s")
        store(1, 0, 256, 3, "s")
        make_f(1, 256, 2)
        store(0, 256, 512, 3, "s")
        synth(0, 256, 512, 0)
        quant_f(1, 256)
        synth(0, 256, 512, 1)
        store(0, 256, 512, 0, "s")
        synth(0, 256, 512, 2)
        store(0, 256, 512, 1, "s")
        store(0, 256, 512, 2, "s")
        synth(1, 256, 384, 0)
        synth(1, 256, 384, 1)
        store(1, 256, 384, 0, "s")
        store(1, 256, 384, 1, "s")
